import numpy as np
import ml_dtypes


def mxq(x, axis, fmt="e4m3"):
    dtype, down = {"e4m3": (ml_dtypes.float8_e4m3fn, 7), "e5m2": (ml_dtypes.float8_e5m2, 14)}[fmt]
    v = np.moveaxis(np.asarray(x, np.float32).astype(ml_dtypes.bfloat16).astype(np.float64), axis, -1)
    blocks = v.reshape(v.shape[:-1] + (-1, 32))
    amax = np.abs(blocks).max(-1, keepdims=True)
    byte = np.maximum(np.where(amax > 0, np.frexp(amax)[1] - 1 + 127, 0) - down, 1)
    scale = np.exp2(byte - 127.0)
    codes = (blocks / scale).astype(np.float32).astype(dtype).astype(np.float64)
    return np.moveaxis((codes * scale).reshape(v.shape), -1, axis)


WIDE = False


def mx_kscale(k):
    if not WIDE:
        return np.ones(k)
    levels = np.array([10, -10, 5, -5, 0])
    if k % 512:
        return np.exp2(np.random.permutation(np.resize(levels, k // 32))).repeat(32)
    a = np.empty((k // 512, 16))
    for p in range(k // 512):
        a[p, :8] = np.random.permutation(np.resize(levels, 8))
        for g in range(8):
            far = levels[np.abs(levels - a[p, g]) >= 10]
            a[p, g + 8] = far[np.random.randint(len(far))]
    return np.exp2(a.ravel()).repeat(32)


def f64(x):
    return np.asarray(x).astype(np.float64)


def striped8(idx):
    return np.asarray(idx).reshape(8, -1, 16).transpose(0, 2, 1).reshape(128, -1).astype(np.uint16)


def unstriped8(offs):
    return offs.reshape(8, 16, -1).transpose(0, 2, 1).reshape(8, -1).astype(np.int64)


def pick8(x, idx, run):
    r = np.arange(len(x))
    return x[r[:, None], idx[r % (8 * run) // run]]


def sigmoid(v):
    return 1.0 / (1.0 + np.exp(-v))


D, T, I, Q, X, E = 512, 2048, 512, 256, 32, 512


def setup_inputs():
    n = np.random.standard_normal
    idx = np.stack([np.random.permutation(T)[:I] for _ in range(8)])
    fd = mx_kscale(D)
    fi = mx_kscale(I)
    ti = np.ones((8, T))
    np.put_along_axis(ti, idx, np.tile(fi, (8, 1)), axis=1)
    return {
        "query": (n((D, Q)) * (np.arange(D)[:, None] // 64 == np.arange(Q) % 8) * 0.0625 * fd[:, None]).astype(np.float32),
        "keys": (n((D, T)) / fd[:, None]).astype(np.float32),
        "size": (np.random.uniform(0.5, 2.0, (1, I)) * fi).astype(np.float32),
        "vals": (n((E, T)) / ti[np.arange(E) % 512 // 64]).astype(np.float32),
        "own": ((np.arange(E)[:, None] // 64 == np.arange(Q) % 8) * 1.0).astype(np.float32),
        "memq": (n((D, Q)) * 1 / np.sqrt(D) * fd[:, None]).astype(np.float32),
        "state": (n((D, E)) * 0.1 / fd[:, None]).astype(np.float32),
        "gb": (n((1, Q))).astype(np.float32),
        "offs": striped8(idx),
    }


def reference(query, keys, size, vals, own, memq, state, gb, offs):
    idx = unstriped8(offs)
    queryq = mxq(f64(query), 0, "e4m3")
    keysidxq = mxq(pick8(f64(keys), idx, 64), 0, "e4m3")
    a = queryq.T @ keysidxq
    p = np.exp(a - np.max(a, axis=1, keepdims=True))
    w = p * f64(size) / np.sum(p, axis=1, keepdims=True)
    wt = w.T
    vt = pick8(f64(vals), idx, 64).T
    vtq = mxq(vt, 0, "e4m3")
    wtq = mxq(wt, 0, "e4m3")
    o = vtq.T @ wtq
    stateq = mxq(f64(state), 0, "e4m3")
    memqq = mxq(f64(memq), 0, "e4m3")
    r = stateq.T @ memqq
    b = (o * sigmoid(f64(gb)) + r * (1.0 - sigmoid(f64(gb)))) * f64(own)
    y = b.reshape(E, X, Q // X).sum(axis=2)
    return y

@@ -1,0 +1,234 @@
+from contextlib import ExitStack
+
+import concourse.mybir as mybir
+from concourse.masks import make_identity
+
+D, T, I, Q, X, E = 512, 2048, 512, 256, 32, 512
+FLOPS = 2 * Q * (D * I + I * E + D * E)
+
+F32 = mybir.dt.float32
+BF16 = mybir.dt.bfloat16
+U32 = mybir.dt.uint32
+U16 = mybir.dt.uint16
+U8 = mybir.dt.uint8
+FP8X4 = mybir.dt.float8_e4m3fn_x4
+ALU = mybir.AluOpType
+ACT = mybir.ActivationFunctionType
+AXIS = mybir.AxisListType
+
+P = 128
+PACK = 4
+QT = Q // P
+GATE_FLOOR = -80.0
+
+
+def tile_attend_ownlists_memory_kernel(tc, query, keys, size, vals, own, memq, state, gb, offs, out):
+    nc = tc.nc
+    with ExitStack() as ctx:
+        sb = ctx.enter_context(tc.tile_pool(name="sb", bufs=1))
+        ps = ctx.enter_context(tc.psum_pool(name="ps", bufs=1))
+
+        def tile(name, shape, dtype, reuse=None):
+            return sb.tile(shape, dtype, name=name, tag=reuse or name, align_bytes=64)
+
+        def mx_tiles(name, width, reuse=None):
+            return tile(name + "_codes", [P, width], U32, reuse), tile(name + "_scales", [P, width], U8)
+
+        def quantize(mx, cols, woven):
+            nc.vector.quantize_mx(out=mx[0][:, cols].bitcast(FP8X4), scales=mx[1][:, cols], in_=woven)
+
+        def matmul(acc, lhs, lhs_cols, rhs, rhs_cols):
+            nc.tensor.matmul_mx(
+                out=acc,
+                lhsT=lhs[0][:, lhs_cols].bitcast(FP8X4),
+                lhsT_scale=lhs[1][:, lhs_cols],
+                rhs=rhs[0][:, rhs_cols].bitcast(FP8X4),
+                rhs_scale=rhs[1][:, rhs_cols],
+                start=True,
+                stop=True,
+            )
+
+        def weave(engine_copy, woven, planes):
+            engine_copy(
+                out=woven.rearrange("p (c i t) -> p c t i", i=4, t=PACK),
+                in_=planes.rearrange("p t (c i) -> p c t i", i=4),
+            )
+
+        def turn(bank, rows, woven):
+            words = rows.bitcast(F32)
+            for u in range(2):
+                nc.tensor.transpose(bank[:, u, :], words[:, u : 2 * P : 2], ident[:])
+            nc.scalar.copy(
+                out=woven.bitcast(F32).rearrange("p (c u) -> p c u", u=2),
+                in_=bank[:].rearrange("p u c -> p c u"),
+            )
+
+        key_planes = keys.rearrange("(p j) t -> j p t", j=PACK)
+        val_planes = vals.rearrange("(p j) t -> j p t", j=PACK)
+        key_pool = [tile("key_pool%d" % j, [P, T], F32) for j in range(PACK)]
+        val_pool = [tile("val_pool%d" % j, [P, T], F32) for j in range(PACK)]
+        offsets = sb.tile([P, I // 16], U16, name="offsets")
+        size_cols = tile("size_cols", [P, PACK], F32)
+        gate_in = tile("gate_in", [P, QT], F32)
+        query_raw = tile("query_raw", [P, PACK, Q], F32)
+        memq_raw = tile("memq_raw", [P, PACK, Q], F32)
+        state_raw = tile("state_raw", [P, PACK, E], F32)
+        own_lo = tile("own_lo", [P, 2 * Q], F32)
+        own_hi = tile("own_hi", [P, 2 * Q], F32)
+
+        nc.sync.dma_start(key_pool[0][:], key_planes[0])
+        nc.sync.dma_start(offsets[:], offs)
+        nc.scalar.dma_start(size_cols[:], size[0].rearrange("(p c) -> p c", c=PACK))
+        with nc.allow_non_contiguous_dma(reason="one gate value a partition"):
+            nc.scalar.dma_start(gate_in[:], gb[0].rearrange("(m p) -> p m", p=P))
+        for j in range(1, PACK):
+            nc.sync.dma_start(key_pool[j][:], key_planes[j])
+        nc.sync.dma_start(query_raw[:], query.rearrange("(p t) q -> p t q", t=PACK))
+        nc.sync.dma_start(state_raw[:], state.rearrange("(p t) e -> p t e", t=PACK))
+        nc.sync.dma_start(val_pool[0][:], val_planes[0])
+        nc.sync.dma_start(memq_raw[:], memq.rearrange("(p t) q -> p t q", t=PACK))
+        for j in range(1, PACK):
+            nc.sync.dma_start(val_pool[j][:], val_planes[j])
+        own_rows = own.rearrange("(p j) q -> p (j q)", j=PACK)
+        nc.sync.dma_start(own_lo[:], own_rows[:, 0 : 2 * Q])
+        nc.sync.dma_start(own_hi[:], own_rows[:, 2 * Q : 4 * Q])
+
+        ident = tile("ident", [P, P], F32)
+        make_identity(nc, ident[:])
+
+        gate_clip = tile("gate_clip", [P, QT], F32)
+        gate_exp = tile("gate_exp", [P, QT], F32)
+        gate_den = tile("gate_den", [P, QT], F32)
+        gate = tile("gate", [P, QT], F32)
+        gate_rest = tile("gate_rest", [P, QT], F32)
+        nc.vector.tensor_scalar(gate_clip[:], gate_in[:], GATE_FLOOR, None, ALU.max)
+        nc.scalar.activation(gate_exp[:], gate_clip[:], ACT.Exp, scale=-1.0)
+        nc.vector.tensor_scalar(gate_den[:], gate_exp[:], 1.0, None, ALU.add)
+        nc.vector.reciprocal(gate[:], gate_den[:])
+        nc.vector.tensor_tensor(gate_rest[:], gate_exp[:], gate[:], ALU.mult)
+
+        size_rows = ps.tile([P, PACK, P], F32, name="size_rows", tag="bank_a")
+        for c in range(PACK):
+            nc.tensor.transpose(size_rows[:, c, :], size_cols[:, c : c + 1].to_broadcast([P, P]), ident[:])
+
+        key_picked = tile("key_picked", [P, PACK, I], BF16)
+        for j in range(PACK):
+            nc.vector.tensor_copy(key_picked[:, j, :], key_pool[j][:].indirect(offsets[:]))
+        key_woven = tile("key_woven", [P, I * PACK], BF16)
+        key_slots = key_woven[:].rearrange("p (i t) -> p i t", t=PACK)
+        for engine_copy, pair in ((nc.scalar.copy, slice(0, 2)), (nc.vector.tensor_copy, slice(2, 4))):
+            engine_copy(out=key_slots[:, :, pair], in_=key_picked[:, pair, :].rearrange("p t i -> p i t"))
+        key_mx = mx_tiles("key", I)
+        quantize(key_mx, slice(0, I), key_woven[:])
+
+        query_woven = tile("query_woven", [P, Q * PACK], BF16)
+        weave(nc.scalar.copy, query_woven[:], query_raw[:])
+        query_mx = mx_tiles("query", Q, "key_picked")
+        quantize(query_mx, slice(0, Q), query_woven[:])
+
+        weight_mx = mx_tiles("weight", Q)
+        weight_woven = tile("weight_woven", [P, Q * PACK], BF16)
+        for m in range(QT):
+            q_cols = slice(m * P, (m + 1) * P)
+            scores = ps.tile([P, I], F32, name="scores%d" % m, tag="bank_b%d" % m)
+            matmul(scores[:], query_mx, q_cols, key_mx, slice(0, I))
+            neg_max = tile("neg_max%d" % m, [P, 1], F32)
+            nc.vector.tensor_reduce(neg_max[:], scores[:], AXIS.X, ALU.max, negate=True)
+            probs = tile("probs%d" % m, [P, I], F32)
+            row_sum = tile("row_sum%d" % m, [P, 1], F32)
+            nc.scalar.activation(probs[:], scores[:], ACT.Exp, bias=neg_max[:], accum_out=row_sum[:])
+            inv_sum = tile("inv_sum%d" % m, [P, 1], F32)
+            nc.vector.reciprocal(inv_sum[:], row_sum[:])
+            weights = tile("weights%d" % m, [P, I], BF16)
+            nc.vector.scalar_tensor_tensor(
+                weights[:].rearrange("p (s c) -> p s c", c=PACK),
+                probs[:].rearrange("p (s c) -> p s c", c=PACK),
+                inv_sum[:],
+                size_rows[:].rearrange("p c s -> p s c"),
+                ALU.mult,
+                ALU.mult,
+            )
+            turned = ps.tile([P, 2, P], F32, name="turned_w%d" % m, tag="bank_t%d" % (m % 2))
+            turn(turned, weights[:], weight_woven[:, m * P * PACK : (m + 1) * P * PACK])
+        quantize(weight_mx, slice(0, Q), weight_woven[:])
+
+        state_lo_mx = mx_tiles("state_lo", E // 2, "neg_max0")
+        state_lo = tile("state_lo", [P, E // 2 * PACK], BF16)
+        weave(nc.scalar.copy, state_lo[:], state_raw[:, :, 0 : E // 2])
+        quantize(state_lo_mx, slice(0, E // 2), state_lo[:])
+        quarter = E // 4
+        state_q2 = tile("state_q2", [P, quarter * PACK], BF16)
+        weave(nc.scalar.copy, state_q2[:], state_raw[:, :, 2 * quarter : 3 * quarter])
+        state_q3 = tile("state_q3", [P, quarter * PACK], BF16, "neg_max1")
+        weave(nc.scalar.copy, state_q3[:], state_raw[:, :, 3 * quarter : E])
+        state_hi_mx = mx_tiles("state_hi", E // 2, "probs0")
+        quantize(state_hi_mx, slice(0, quarter), state_q2[:])
+        quantize(state_hi_mx, slice(quarter, 2 * quarter), state_q3[:])
+        memq_woven = tile("memq_woven", [P, Q * PACK], BF16, "weights0")
+        weave(nc.scalar.copy, memq_woven[:], memq_raw[:])
+        memq_mx = mx_tiles("memq", Q)
+        quantize(memq_mx, slice(0, Q), memq_woven[:])
+        mem_gated = []
+        for m in range(QT):
+            mem_read = ps.tile([P, E], F32, name="mem_read%d" % m, tag="bank_b%d" % m)
+            for half, state_mx in enumerate((state_lo_mx, state_hi_mx)):
+                e_cols = slice(half * E // 2, (half + 1) * E // 2)
+                matmul(mem_read[:, e_cols], memq_mx, slice(m * P, (m + 1) * P), state_mx, slice(0, E // 2))
+            gated = tile("mem_gated%d" % m, [P, PACK, P], F32)
+            nc.scalar.activation(
+                gated[:], mem_read[:].rearrange("q (p j) -> q j p", j=PACK), ACT.Copy, scale=gate_rest[:, m : m + 1]
+            )
+            mem_gated.append(gated)
+
+        result = tile("result", [P, PACK, X], F32)
+
+        def pick(j, reuse):
+            val_picked = tile("val_picked%d" % j, [P, I], BF16, reuse)
+            nc.vector.tensor_copy(val_picked[:], val_pool[j][:].indirect(offsets[:]))
+            turned = ps.tile([P, 2, P], F32, name="turned_v%d" % j, tag="bank_t%d" % (j % 2))
+            val_woven = tile("val_woven%d" % j, [P, P * PACK], BF16)
+            turn(turned, val_picked[:], val_woven[:])
+            return val_woven
+
+        def attend(j, val_woven, reuse, bank):
+            val_mx = mx_tiles("val%d" % j, P, reuse)
+            quantize(val_mx, slice(0, P), val_woven[:])
+            attn = ps.tile([P, QT, P], F32, name="attn%d" % j, tag=bank)
+            attn_gated = tile("attn_gated%d" % j, [P, QT, P], F32)
+            for m in range(QT):
+                matmul(attn[:, m, :], weight_mx, slice(m * P, (m + 1) * P), val_mx, slice(0, P))
+            for m in range(QT):
+                nc.scalar.activation(attn_gated[:, m, :], attn[:, m, :], ACT.Copy, scale=gate[:, m : m + 1])
+            return attn_gated
+
+        def mix(j, attn_gated, mixed):
+            for m in range(QT):
+                q_cols = slice(m * P, (m + 1) * P)
+                nc.tensor.matmul(mixed[:, q_cols], mem_gated[m][:, j, :], ident[:], start=True, stop=False, is_transpose=True)
+                nc.tensor.matmul(mixed[:, q_cols], attn_gated[:, m, :], ident[:], start=False, stop=True, is_transpose=True)
+
+        def mask(name, mixed, own_part, reuse):
+            masked = tile(name, list(mixed.shape), F32, reuse)
+            nc.vector.tensor_tensor(masked[:], mixed, own_part, ALU.mult)
+            return masked
+
+        def place_sums(masked, sums):
+            nc.vector.tensor_reduce(sums, masked.rearrange("p (x k) -> p x k", k=Q // X), AXIS.X, ALU.add)
+
+        woven0 = pick(0, "probs1")
+        woven1 = pick(1, "weights1")
+        mixed01 = ps.tile([P, 2 * Q], F32, name="mixed01", tag="bank_a")
+        mix(0, attend(0, woven0, None, "bank_o"), mixed01[:, 0:Q])
+        woven2 = pick(2, "weights0")
+        mix(1, attend(1, woven1, None, "bank_o"), mixed01[:, Q : 2 * Q])
+        woven3 = pick(3, "val_woven1")
+        gated2 = attend(2, woven2, "val_pool3", "bank_o")
+        masked01 = mask("masked01", mixed01[:], own_lo[:], "val_woven2")
+        gated3 = attend(3, woven3, "own_lo", "bank_b0")
+        place_sums(masked01[:], result[:, 0:2, :].rearrange("p j x -> p (j x)"))
+        for j, gated in ((2, gated2), (3, gated3)):
+            mixed = ps.tile([P, Q], F32, name="mixed%d" % j, tag="bank_c%d" % j)
+            mix(j, gated, mixed[:])
+            masked = mask("masked%d" % j, mixed[:], own_hi[:, (j - 2) * Q : (j - 1) * Q], None)
+            place_sums(masked[:], result[:, j, :])
+        nc.sync.dma_start(out.rearrange("(p j) x -> p j x", j=PACK), result[:])

@@ -20,19 +20,27 @@ P = 128
 PACK = 4
 QT = Q // P
 GATE_FLOOR = -80.0
+POOL_BYTES = 4 * T
 
 
 def tile_attend_ownlists_memory_kernel(tc, query, keys, size, vals, own, memq, state, gb, offs, out):
     nc = tc.nc
     with ExitStack() as ctx:
         sb = ctx.enter_context(tc.tile_pool(name="sb", bufs=1))
+        vb = ctx.enter_context(tc.tile_pool(name="vb", bufs=1))
         ps = ctx.enter_context(tc.psum_pool(name="ps", bufs=1))
 
         def tile(name, shape, dtype, reuse=None):
             return sb.tile(shape, dtype, name=name, tag=reuse or name, align_bytes=64)
 
-        def mx_tiles(name, width, reuse=None):
-            return tile(name + "_codes", [P, width], U32, reuse), tile(name + "_scales", [P, width], U8)
+        def in_pool(j, at, name, shape, dtype):
+            return vb.tile(shape, dtype, name=name, offset=j * POOL_BYTES + at, align_bytes=64)
+
+        def mx_tiles(name, width, reuse=None, pool=None, at=0):
+            scales = tile(name + "_scales", [P, width], U8)
+            if pool is None:
+                return tile(name + "_codes", [P, width], U32, reuse), scales
+            return in_pool(pool, at, name + "_codes", [P, width], U32), scales
 
         def quantize(mx, cols, woven):
             nc.vector.quantize_mx(out=mx[0][:, cols].bitcast(FP8X4), scales=mx[1][:, cols], in_=woven)
@@ -66,7 +74,7 @@ def tile_attend_ownlists_memory_kernel(tc, query, keys, size, vals, own, memq, s
         key_planes = keys.rearrange("(p j) t -> j p t", j=PACK)
         val_planes = vals.rearrange("(p j) t -> j p t", j=PACK)
         key_pool = [tile("key_pool%d" % j, [P, T], F32) for j in range(PACK)]
-        val_pool = [tile("val_pool%d" % j, [P, T], F32) for j in range(PACK)]
+        val_pool = [in_pool(j, 0, "val_pool%d" % j, [P, T], F32) for j in range(PACK)]
         offsets = sb.tile([P, I // 16], U16, name="offsets")
         size_cols = tile("size_cols", [P, PACK], F32)
         gate_in = tile("gate_in", [P, QT], F32)
@@ -84,9 +92,9 @@ def tile_attend_ownlists_memory_kernel(tc, query, keys, size, vals, own, memq, s
         for j in range(1, PACK):
             nc.sync.dma_start(key_pool[j][:], key_planes[j])
         nc.sync.dma_start(query_raw[:], query.rearrange("(p t) q -> p t q", t=PACK))
-        nc.sync.dma_start(state_raw[:], state.rearrange("(p t) e -> p t e", t=PACK))
-        nc.sync.dma_start(val_pool[0][:], val_planes[0])
         nc.sync.dma_start(memq_raw[:], memq.rearrange("(p t) q -> p t q", t=PACK))
+        nc.sync.dma_start(val_pool[0][:], val_planes[0])
+        nc.sync.dma_start(state_raw[:], state.rearrange("(p t) e -> p t e", t=PACK))
         for j in range(1, PACK):
             nc.sync.dma_start(val_pool[j][:], val_planes[j])
         own_rows = own.rearrange("(p j) q -> p (j q)", j=PACK)
@@ -118,94 +126,98 @@ def tile_attend_ownlists_memory_kernel(tc, query, keys, size, vals, own, memq, s
         key_slots = key_woven[:].rearrange("p (i t) -> p i t", t=PACK)
         for engine_copy, pair in ((nc.scalar.copy, slice(0, 2)), (nc.vector.tensor_copy, slice(2, 4))):
             engine_copy(out=key_slots[:, :, pair], in_=key_picked[:, pair, :].rearrange("p t i -> p i t"))
-        key_mx = mx_tiles("key", I)
-        quantize(key_mx, slice(0, I), key_woven[:])
+        query_mx = []
+        for m, reuse in enumerate(("key_pool3", "key_picked")):
+            query_woven = tile("query_woven%d" % m, [P, P * PACK], BF16)
+            weave(nc.scalar.copy, query_woven[:], query_raw[:, :, m * P : (m + 1) * P])
+            query_mx.append(mx_tiles("query%d" % m, P, reuse))
+            quantize(query_mx[m], slice(0, P), query_woven[:])
+            if m == 0:
+                key_mx = mx_tiles("key", I)
+                quantize(key_mx, slice(0, I), key_woven[:])
 
-        query_woven = tile("query_woven", [P, Q * PACK], BF16)
-        weave(nc.scalar.copy, query_woven[:], query_raw[:])
-        query_mx = mx_tiles("query", Q, "key_picked")
-        quantize(query_mx, slice(0, Q), query_woven[:])
-
-        weight_mx = mx_tiles("weight", Q)
-        weight_woven = tile("weight_woven", [P, Q * PACK], BF16)
+        row_sum = tile("row_sum", [P, QT], F32)
+        probs = []
         for m in range(QT):
-            q_cols = slice(m * P, (m + 1) * P)
             scores = ps.tile([P, I], F32, name="scores%d" % m, tag="bank_b%d" % m)
-            matmul(scores[:], query_mx, q_cols, key_mx, slice(0, I))
+            matmul(scores[:], query_mx[m], slice(0, P), key_mx, slice(0, I))
             neg_max = tile("neg_max%d" % m, [P, 1], F32)
             nc.vector.tensor_reduce(neg_max[:], scores[:], AXIS.X, ALU.max, negate=True)
-            probs = tile("probs%d" % m, [P, I], F32)
-            row_sum = tile("row_sum%d" % m, [P, 1], F32)
-            nc.scalar.activation(probs[:], scores[:], ACT.Exp, bias=neg_max[:], accum_out=row_sum[:])
-            inv_sum = tile("inv_sum%d" % m, [P, 1], F32)
-            nc.vector.reciprocal(inv_sum[:], row_sum[:])
+            probs.append(tile("probs%d" % m, [P, I], F32))
+            nc.scalar.activation(probs[m][:], scores[:], ACT.Exp, bias=neg_max[:], accum_out=row_sum[:, m : m + 1])
+
+        memq_woven = tile("memq_woven", [P, Q * PACK], BF16)
+        weave(nc.scalar.copy, memq_woven[:], memq_raw[:])
+        state_woven = tile("state_woven", [P, E * PACK], BF16)
+        for half in range(2):
+            weave(
+                nc.scalar.copy,
+                state_woven[:, half * E // 2 * PACK : (half + 1) * E // 2 * PACK],
+                state_raw[:, :, half * E // 2 : (half + 1) * E // 2],
+            )
+
+        def pick(j, reuse=None):
+            val_picked = tile("val_picked%d" % j, [P, I], BF16, reuse)
+            nc.vector.tensor_copy(val_picked[:], val_pool[j][:].indirect(offsets[:]))
+            return val_picked
+
+        def turn_values(j, val_picked, woven):
+            turned = ps.tile([P, 2, P], F32, name="turned_v%d" % j, tag="bank_t%d" % (j % 2))
+            turn(turned, val_picked[:], woven)
+
+        picked0 = pick(0)
+        inv_sum = tile("inv_sum", [P, QT], F32)
+        nc.vector.reciprocal(inv_sum[:], row_sum[:])
+        memq_mx = mx_tiles("memq", Q, pool=0)
+        quantize(memq_mx, slice(0, Q), memq_woven[:])
+        weight_woven = tile("weight_woven", [P, Q * PACK], BF16, "state_raw")
+        for m in range(QT):
             weights = tile("weights%d" % m, [P, I], BF16)
             nc.vector.scalar_tensor_tensor(
                 weights[:].rearrange("p (s c) -> p s c", c=PACK),
-                probs[:].rearrange("p (s c) -> p s c", c=PACK),
-                inv_sum[:],
+                probs[m][:].rearrange("p (s c) -> p s c", c=PACK),
+                inv_sum[:, m : m + 1],
                 size_rows[:].rearrange("p c s -> p s c"),
                 ALU.mult,
                 ALU.mult,
             )
             turned = ps.tile([P, 2, P], F32, name="turned_w%d" % m, tag="bank_t%d" % (m % 2))
             turn(turned, weights[:], weight_woven[:, m * P * PACK : (m + 1) * P * PACK])
-        quantize(weight_mx, slice(0, Q), weight_woven[:])
 
-        state_lo_mx = mx_tiles("state_lo", E // 2, "neg_max0")
-        state_lo = tile("state_lo", [P, E // 2 * PACK], BF16)
-        weave(nc.scalar.copy, state_lo[:], state_raw[:, :, 0 : E // 2])
-        quantize(state_lo_mx, slice(0, E // 2), state_lo[:])
-        quarter = E // 4
-        state_q2 = tile("state_q2", [P, quarter * PACK], BF16)
-        weave(nc.scalar.copy, state_q2[:], state_raw[:, :, 2 * quarter : 3 * quarter])
-        state_q3 = tile("state_q3", [P, quarter * PACK], BF16, "neg_max1")
-        weave(nc.scalar.copy, state_q3[:], state_raw[:, :, 3 * quarter : E])
-        state_hi_mx = mx_tiles("state_hi", E // 2, "probs0")
-        quantize(state_hi_mx, slice(0, quarter), state_q2[:])
-        quantize(state_hi_mx, slice(quarter, 2 * quarter), state_q3[:])
-        memq_woven = tile("memq_woven", [P, Q * PACK], BF16, "weights0")
-        weave(nc.scalar.copy, memq_woven[:], memq_raw[:])
-        memq_mx = mx_tiles("memq", Q)
-        quantize(memq_mx, slice(0, Q), memq_woven[:])
-        mem_gated = []
-        for m in range(QT):
-            mem_read = ps.tile([P, E], F32, name="mem_read%d" % m, tag="bank_b%d" % m)
-            for half, state_mx in enumerate((state_lo_mx, state_hi_mx)):
-                e_cols = slice(half * E // 2, (half + 1) * E // 2)
-                matmul(mem_read[:, e_cols], memq_mx, slice(m * P, (m + 1) * P), state_mx, slice(0, E // 2))
-            gated = tile("mem_gated%d" % m, [P, PACK, P], F32)
-            nc.scalar.activation(
-                gated[:], mem_read[:].rearrange("q (p j) -> q j p", j=PACK), ACT.Copy, scale=gate_rest[:, m : m + 1]
-            )
-            mem_gated.append(gated)
+        half_e = E // 2
+        state_mx = [mx_tiles("state_lo", half_e)]
+        quantize(state_mx[0], slice(0, half_e), state_woven[:, 0 : half_e * PACK])
+        picked1 = pick(1)
+        state_mx.append(mx_tiles("state_hi", half_e, pool=1))
+        quantize(state_mx[1], slice(0, half_e), state_woven[:, half_e * PACK : E * PACK])
+        weight_mx = mx_tiles("weight", Q)
+        quantize(weight_mx, slice(0, Q), weight_woven[:])
+        woven01 = tile("val_woven01", [P, 2 * P * PACK], BF16)
+        turn_values(0, picked0, woven01[:, 0 : P * PACK])
+        turn_values(1, picked1, woven01[:, P * PACK : 2 * P * PACK])
 
         result = tile("result", [P, PACK, X], F32)
 
-        def pick(j, reuse):
-            val_picked = tile("val_picked%d" % j, [P, I], BF16, reuse)
-            nc.vector.tensor_copy(val_picked[:], val_pool[j][:].indirect(offsets[:]))
-            turned = ps.tile([P, 2, P], F32, name="turned_v%d" % j, tag="bank_t%d" % (j % 2))
-            val_woven = tile("val_woven%d" % j, [P, P * PACK], BF16)
-            turn(turned, val_picked[:], val_woven[:])
-            return val_woven
-
-        def attend(j, val_woven, reuse, bank):
-            val_mx = mx_tiles("val%d" % j, P, reuse)
-            quantize(val_mx, slice(0, P), val_woven[:])
-            attn = ps.tile([P, QT, P], F32, name="attn%d" % j, tag=bank)
-            attn_gated = tile("attn_gated%d" % j, [P, QT, P], F32)
+        def attend(name, val_woven, width, val_mx, bank):
+            quantize(val_mx, slice(0, width), val_woven[:])
+            attn = ps.tile([P, QT, width], F32, name=name + "_attn", tag=bank)
             for m in range(QT):
-                matmul(attn[:, m, :], weight_mx, slice(m * P, (m + 1) * P), val_mx, slice(0, P))
+                matmul(attn[:, m, :], weight_mx, slice(m * P, (m + 1) * P), val_mx, slice(0, width))
+            return attn
+
+        def gate_attn(attn, attn_gated):
             for m in range(QT):
                 nc.scalar.activation(attn_gated[:, m, :], attn[:, m, :], ACT.Copy, scale=gate[:, m : m + 1])
-            return attn_gated
 
-        def mix(j, attn_gated, mixed):
-            for m in range(QT):
-                q_cols = slice(m * P, (m + 1) * P)
-                nc.tensor.matmul(mixed[:, q_cols], mem_gated[m][:, j, :], ident[:], start=True, stop=False, is_transpose=True)
-                nc.tensor.matmul(mixed[:, q_cols], attn_gated[:, m, :], ident[:], start=False, stop=True, is_transpose=True)
+        mem_reads = []
+        for m in range(QT):
+            mem_reads.append(ps.tile([P, E], F32, name="mem_read%d" % m, tag="bank_b%d" % m))
+            for half in range(2):
+                e_cols = slice(half * half_e, (half + 1) * half_e)
+                matmul(mem_reads[m][:, e_cols], memq_mx, slice(m * P, (m + 1) * P), state_mx[half], slice(0, half_e))
+
+        def add_turned(mixed, block, start, stop):
+            nc.tensor.matmul(mixed, block, ident[:], start=start, stop=stop, is_transpose=True)
 
         def mask(name, mixed, own_part, reuse):
             masked = tile(name, list(mixed.shape), F32, reuse)
@@ -215,20 +227,40 @@ def tile_attend_ownlists_memory_kernel(tc, query, keys, size, vals, own, memq, s
         def place_sums(masked, sums):
             nc.vector.tensor_reduce(sums, masked.rearrange("p (x k) -> p x k", k=Q // X), AXIS.X, ALU.add)
 
-        woven0 = pick(0, "probs1")
-        woven1 = pick(1, "weights1")
-        mixed01 = ps.tile([P, 2 * Q], F32, name="mixed01", tag="bank_a")
-        mix(0, attend(0, woven0, None, "bank_o"), mixed01[:, 0:Q])
-        woven2 = pick(2, "weights0")
-        mix(1, attend(1, woven1, None, "bank_o"), mixed01[:, Q : 2 * Q])
-        woven3 = pick(3, "val_woven1")
-        gated2 = attend(2, woven2, "val_pool3", "bank_o")
-        masked01 = mask("masked01", mixed01[:], own_lo[:], "val_woven2")
-        gated3 = attend(3, woven3, "own_lo", "bank_b0")
+        picked2 = pick(2)
+        woven2 = tile("val_woven2", [P, P * PACK], BF16)
+        turn_values(2, picked2, woven2[:])
+        attn01 = attend("val01", woven01, 2 * P, mx_tiles("val01", 2 * P, pool=2), "bank_o")
+        mixed01 = ps.tile([P, 2, Q], F32, name="mixed01", tag="bank_a")
+        mixed2 = ps.tile([P, Q], F32, name="mixed2", tag="bank_c2")
+        mixed3 = ps.tile([P, Q], F32, name="mixed3", tag="bank_c3")
+        mixed = [mixed01[:, 0, :], mixed01[:, 1, :], mixed2[:], mixed3[:]]
+        for m in range(QT):
+            mem_gated = tile("mem_gated0", [P, PACK, P], F32, "val_picked1") if m == 0 else in_pool(2, 2048, "mem_gated1", [P, PACK, P], F32)
+            nc.scalar.activation(
+                mem_gated[:], mem_reads[m][:].rearrange("q (p j) -> q j p", j=PACK), ACT.Copy, scale=gate_rest[:, m : m + 1]
+            )
+            for j in range(PACK):
+                add_turned(mixed[j][:, m * P : (m + 1) * P], mem_gated[:, j, :], m == 0 and j != 1, False)
+        picked3 = pick(3)
+        woven3 = tile("val_woven3", [P, P * PACK], BF16)
+        turn_values(3, picked3, woven3[:])
+        gated01 = in_pool(3, 4 * P, "gated01", [P, QT, 2 * P], F32)
+        gate_attn(attn01, gated01)
+        attn2 = attend("val2", woven2, P, mx_tiles("val2", P, pool=3), "bank_b0")
+        attn3 = attend("val3", woven3, P, mx_tiles("val3", P), "bank_b1")
+        gated2 = tile("gated2", [P, QT, P], F32)
+        gate_attn(attn2, gated2)
+        gated3 = tile("gated3", [P, QT, P], F32)
+        gate_attn(attn3, gated3)
+        for m in range(QT):
+            for j in range(2):
+                add_turned(mixed[j][:, m * P : (m + 1) * P], gated01[:, m, j * P : (j + 1) * P], False, m == 1 and j == 1)
+        masked01 = mask("masked01", mixed01[:].rearrange("p j q -> p (j q)"), own_lo[:], None)
         place_sums(masked01[:], result[:, 0:2, :].rearrange("p j x -> p (j x)"))
         for j, gated in ((2, gated2), (3, gated3)):
-            mixed = ps.tile([P, Q], F32, name="mixed%d" % j, tag="bank_c%d" % j)
-            mix(j, gated, mixed[:])
-            masked = mask("masked%d" % j, mixed[:], own_hi[:, (j - 2) * Q : (j - 1) * Q], None)
+            for m in range(QT):
+                add_turned(mixed[j][:, m * P : (m + 1) * P], gated[:, m, :], False, m == 1)
+            masked = mask("masked%d" % j, mixed[j], own_hi[:, (j - 2) * Q : (j - 1) * Q], None)
             place_sums(masked[:], result[:, j, :])
         nc.sync.dma_start(out.rearrange("(p j) x -> p j x", j=PACK), result[:])

@@ -80,7 +80,8 @@ def tile_attend_ownlists_memory_kernel(tc, query, keys, size, vals, own, memq, s
         gate_in = tile("gate_in", [P, QT], F32)
         query_raw = tile("query_raw", [P, PACK, Q], F32)
         memq_raw = tile("memq_raw", [P, PACK, Q], F32)
-        state_raw = tile("state_raw", [P, PACK, E], F32)
+        state_raw = [tile("state_raw%d" % u, [P, 2, E], F32) for u in range(2)]
+        state_pairs = state.rearrange("(p u t) e -> u p t e", u=2, t=2)
         own_lo = tile("own_lo", [P, 2 * Q], F32)
         own_hi = tile("own_hi", [P, 2 * Q], F32)
 
@@ -93,8 +94,9 @@ def tile_attend_ownlists_memory_kernel(tc, query, keys, size, vals, own, memq, s
             nc.sync.dma_start(key_pool[j][:], key_planes[j])
         nc.sync.dma_start(query_raw[:], query.rearrange("(p t) q -> p t q", t=PACK))
         nc.sync.dma_start(memq_raw[:], memq.rearrange("(p t) q -> p t q", t=PACK))
+        nc.sync.dma_start(state_raw[0][:], state_pairs[0])
         nc.sync.dma_start(val_pool[0][:], val_planes[0])
-        nc.sync.dma_start(state_raw[:], state.rearrange("(p t) e -> p t e", t=PACK))
+        nc.sync.dma_start(state_raw[1][:], state_pairs[1])
         for j in range(1, PACK):
             nc.sync.dma_start(val_pool[j][:], val_planes[j])
         own_rows = own.rearrange("(p j) q -> p (j q)", j=PACK)
@@ -136,25 +138,25 @@ def tile_attend_ownlists_memory_kernel(tc, query, keys, size, vals, own, memq, s
                 key_mx = mx_tiles("key", I)
                 quantize(key_mx, slice(0, I), key_woven[:])
 
+        memq_woven = tile("memq_woven", [P, Q * PACK], BF16)
+        weave(nc.scalar.copy, memq_woven[:], memq_raw[:])
+        state_woven = tile("state_woven", [P, E, PACK], BF16)
+
+        def weave_pair(u):
+            nc.scalar.copy(out=state_woven[:, :, 2 * u : 2 * u + 2], in_=state_raw[u][:].rearrange("p t e -> p e t"))
+
+        weave_pair(0)
         row_sum = tile("row_sum", [P, QT], F32)
-        probs = []
+        probs_both = tile("probs", [P, QT, I], F32, "state_raw0")
+        probs = [probs_both[:, m, :] for m in range(QT)]
         for m in range(QT):
             scores = ps.tile([P, I], F32, name="scores%d" % m, tag="bank_b%d" % m)
             matmul(scores[:], query_mx[m], slice(0, P), key_mx, slice(0, I))
             neg_max = tile("neg_max%d" % m, [P, 1], F32)
             nc.vector.tensor_reduce(neg_max[:], scores[:], AXIS.X, ALU.max, negate=True)
-            probs.append(tile("probs%d" % m, [P, I], F32))
             nc.scalar.activation(probs[m][:], scores[:], ACT.Exp, bias=neg_max[:], accum_out=row_sum[:, m : m + 1])
 
-        memq_woven = tile("memq_woven", [P, Q * PACK], BF16)
-        weave(nc.scalar.copy, memq_woven[:], memq_raw[:])
-        state_woven = tile("state_woven", [P, E * PACK], BF16)
-        for half in range(2):
-            weave(
-                nc.scalar.copy,
-                state_woven[:, half * E // 2 * PACK : (half + 1) * E // 2 * PACK],
-                state_raw[:, :, half * E // 2 : (half + 1) * E // 2],
-            )
+        weave_pair(1)
 
         def pick(j, reuse=None):
             val_picked = tile("val_picked%d" % j, [P, I], BF16, reuse)
@@ -162,15 +164,16 @@ def tile_attend_ownlists_memory_kernel(tc, query, keys, size, vals, own, memq, s
             return val_picked
 
         def turn_values(j, val_picked, woven):
-            turned = ps.tile([P, 2, P], F32, name="turned_v%d" % j, tag="bank_t%d" % (j % 2))
+            turned = ps.tile([P, 2, P], F32, name="turned_v%d" % j, tag=("bank_o", "bank_t1", "bank_t0", "bank_t1")[j])
             turn(turned, val_picked[:], woven)
 
         picked0 = pick(0)
-        inv_sum = tile("inv_sum", [P, QT], F32)
+        inv_sum = in_pool(0, 4096, "inv_sum", [P, QT], F32)
         nc.vector.reciprocal(inv_sum[:], row_sum[:])
         memq_mx = mx_tiles("memq", Q, pool=0)
         quantize(memq_mx, slice(0, Q), memq_woven[:])
-        weight_woven = tile("weight_woven", [P, Q * PACK], BF16, "state_raw")
+        turned_woven = tile("turned_woven", [P, (Q + 2 * P) * PACK], BF16, "state_raw1")
+        weight_woven = turned_woven[:, 0 : Q * PACK]
         for m in range(QT):
             weights = tile("weights%d" % m, [P, I], BF16)
             nc.vector.scalar_tensor_tensor(
@@ -184,15 +187,12 @@ def tile_attend_ownlists_memory_kernel(tc, query, keys, size, vals, own, memq, s
             turned = ps.tile([P, 2, P], F32, name="turned_w%d" % m, tag="bank_t%d" % (m % 2))
             turn(turned, weights[:], weight_woven[:, m * P * PACK : (m + 1) * P * PACK])
 
-        half_e = E // 2
-        state_mx = [mx_tiles("state_lo", half_e)]
-        quantize(state_mx[0], slice(0, half_e), state_woven[:, 0 : half_e * PACK])
+        state_mx = mx_tiles("state", E)
+        quantize(state_mx, slice(0, E), state_woven[:].rearrange("p e t -> p (e t)"))
         picked1 = pick(1)
-        state_mx.append(mx_tiles("state_hi", half_e, pool=1))
-        quantize(state_mx[1], slice(0, half_e), state_woven[:, half_e * PACK : E * PACK])
-        weight_mx = mx_tiles("weight", Q)
+        weight_mx = mx_tiles("weight", Q, pool=1)
         quantize(weight_mx, slice(0, Q), weight_woven[:])
-        woven01 = tile("val_woven01", [P, 2 * P * PACK], BF16)
+        woven01 = turned_woven[:, Q * PACK : (Q + 2 * P) * PACK]
         turn_values(0, picked0, woven01[:, 0 : P * PACK])
         turn_values(1, picked1, woven01[:, P * PACK : 2 * P * PACK])
 
@@ -212,9 +212,7 @@ def tile_attend_ownlists_memory_kernel(tc, query, keys, size, vals, own, memq, s
         mem_reads = []
         for m in range(QT):
             mem_reads.append(ps.tile([P, E], F32, name="mem_read%d" % m, tag="bank_b%d" % m))
-            for half in range(2):
-                e_cols = slice(half * half_e, (half + 1) * half_e)
-                matmul(mem_reads[m][:, e_cols], memq_mx, slice(m * P, (m + 1) * P), state_mx[half], slice(0, half_e))
+            matmul(mem_reads[m][:], memq_mx, slice(m * P, (m + 1) * P), state_mx, slice(0, E))
 
         def add_turned(mixed, block, start, stop):
             nc.tensor.matmul(mixed, block, ident[:], start=start, stop=stop, is_transpose=True)
@@ -236,7 +234,7 @@ def tile_attend_ownlists_memory_kernel(tc, query, keys, size, vals, own, memq, s
         mixed3 = ps.tile([P, Q], F32, name="mixed3", tag="bank_c3")
         mixed = [mixed01[:, 0, :], mixed01[:, 1, :], mixed2[:], mixed3[:]]
         for m in range(QT):
-            mem_gated = tile("mem_gated0", [P, PACK, P], F32, "val_picked1") if m == 0 else in_pool(2, 2048, "mem_gated1", [P, PACK, P], F32)
+            mem_gated = tile("mem_gated0", [P, PACK, P], F32) if m == 0 else in_pool(2, 2048, "mem_gated1", [P, PACK, P], F32)
             nc.scalar.activation(
                 mem_gated[:], mem_reads[m][:].rearrange("q (p j) -> q j p", j=PACK), ACT.Copy, scale=gate_rest[:, m : m + 1]
             )
@@ -248,19 +246,26 @@ def tile_attend_ownlists_memory_kernel(tc, query, keys, size, vals, own, memq, s
         gated01 = in_pool(3, 4 * P, "gated01", [P, QT, 2 * P], F32)
         gate_attn(attn01, gated01)
         attn2 = attend("val2", woven2, P, mx_tiles("val2", P, pool=3), "bank_b0")
-        attn3 = attend("val3", woven3, P, mx_tiles("val3", P), "bank_b1")
-        gated2 = tile("gated2", [P, QT, P], F32)
+        val3_mx = mx_tiles("val3", P)
+        quantize(val3_mx, slice(0, P), woven3[:])
+        attn3 = [ps.tile([P, P], F32, name="attn3_%d" % m, tag=("bank_b1", "bank_t0")[m]) for m in range(QT)]
+        for m in range(QT):
+            matmul(attn3[m][:], weight_mx, slice(m * P, (m + 1) * P), val3_mx, slice(0, P))
+        gated2 = tile("gated2", [P, QT, P], F32, "val_woven3")
         gate_attn(attn2, gated2)
         gated3 = tile("gated3", [P, QT, P], F32)
-        gate_attn(attn3, gated3)
+        for m in range(QT):
+            nc.scalar.activation(gated3[:, m, :], attn3[m][:], ACT.Copy, scale=gate[:, m : m + 1])
         for m in range(QT):
             for j in range(2):
                 add_turned(mixed[j][:, m * P : (m + 1) * P], gated01[:, m, j * P : (j + 1) * P], False, m == 1 and j == 1)
         masked01 = mask("masked01", mixed01[:].rearrange("p j q -> p (j q)"), own_lo[:], None)
         place_sums(masked01[:], result[:, 0:2, :].rearrange("p j x -> p (j x)"))
+        out_rows = out.rearrange("(p j) x -> p j x", j=PACK)
+        nc.sync.dma_start(out_rows[:, 0:2, :], result[:, 0:2, :])
         for j, gated in ((2, gated2), (3, gated3)):
             for m in range(QT):
                 add_turned(mixed[j][:, m * P : (m + 1) * P], gated[:, m, :], False, m == 1)
             masked = mask("masked%d" % j, mixed[j], own_hi[:, (j - 2) * Q : (j - 1) * Q], None)
             place_sums(masked[:], result[:, j, :])
-        nc.sync.dma_start(out.rearrange("(p j) x -> p j x", j=PACK), result[:])
+        nc.sync.dma_start(out_rows[:, 2:4, :], result[:, 2:4, :])

from contextlib import ExitStack

import concourse.mybir as mybir
from concourse.masks import make_identity

D, T, I, Q, X, E = 512, 2048, 512, 256, 32, 512
FLOPS = 2 * Q * (D * I + I * E + D * E)

F32 = mybir.dt.float32
BF16 = mybir.dt.bfloat16
U32 = mybir.dt.uint32
U16 = mybir.dt.uint16
U8 = mybir.dt.uint8
FP8X4 = mybir.dt.float8_e4m3fn_x4
ALU = mybir.AluOpType
ACT = mybir.ActivationFunctionType
AXIS = mybir.AxisListType

P = 128
PACK = 4
QT = Q // P
GATE_FLOOR = -80.0
POOL_BYTES = 4 * T


def tile_attend_ownlists_memory_kernel(tc, query, keys, size, vals, own, memq, state, gb, offs, out):
    nc = tc.nc
    with ExitStack() as ctx:
        sb = ctx.enter_context(tc.tile_pool(name="sb", bufs=1))
        vb = ctx.enter_context(tc.tile_pool(name="vb", bufs=1))
        ps = ctx.enter_context(tc.psum_pool(name="ps", bufs=1))

        def tile(name, shape, dtype, reuse=None):
            return sb.tile(shape, dtype, name=name, tag=reuse or name, align_bytes=64)

        def in_pool(j, at, name, shape, dtype):
            return vb.tile(shape, dtype, name=name, offset=j * POOL_BYTES + at, align_bytes=64)

        def mx_tiles(name, width, reuse=None, pool=None, at=0):
            scales = tile(name + "_scales", [P, width], U8)
            if pool is None:
                return tile(name + "_codes", [P, width], U32, reuse), scales
            return in_pool(pool, at, name + "_codes", [P, width], U32), scales

        def quantize(mx, cols, woven):
            nc.vector.quantize_mx(out=mx[0][:, cols].bitcast(FP8X4), scales=mx[1][:, cols], in_=woven)

        def matmul(acc, lhs, lhs_cols, rhs, rhs_cols):
            nc.tensor.matmul_mx(
                out=acc,
                lhsT=lhs[0][:, lhs_cols].bitcast(FP8X4),
                lhsT_scale=lhs[1][:, lhs_cols],
                rhs=rhs[0][:, rhs_cols].bitcast(FP8X4),
                rhs_scale=rhs[1][:, rhs_cols],
                start=True,
                stop=True,
            )

        def weave(engine_copy, woven, planes):
            engine_copy(
                out=woven.rearrange("p (c i t) -> p c t i", i=4, t=PACK),
                in_=planes.rearrange("p t (c i) -> p c t i", i=4),
            )

        def turn(bank, rows, woven):
            words = rows.bitcast(F32)
            for u in range(2):
                nc.tensor.transpose(bank[:, u, :], words[:, u : 2 * P : 2], ident[:])
            nc.scalar.copy(
                out=woven.bitcast(F32).rearrange("p (c u) -> p c u", u=2),
                in_=bank[:].rearrange("p u c -> p c u"),
            )

        key_planes = keys.rearrange("(p j) t -> j p t", j=PACK)
        val_planes = vals.rearrange("(p j) t -> j p t", j=PACK)
        key_pool = [tile("key_pool%d" % j, [P, T], F32) for j in range(PACK)]
        val_pool = [in_pool(j, 0, "val_pool%d" % j, [P, T], F32) for j in range(PACK)]
        offsets = sb.tile([P, I // 16], U16, name="offsets")
        size_cols = tile("size_cols", [P, PACK], F32)
        gate_in = tile("gate_in", [P, QT], F32)
        query_raw = tile("query_raw", [P, PACK, Q], F32)
        memq_raw = tile("memq_raw", [P, PACK, Q], F32)
        state_raw = [tile("state_raw%d" % u, [P, 2, E], F32) for u in range(2)]
        state_pairs = state.rearrange("(p u t) e -> u p t e", u=2, t=2)
        own_lo = tile("own_lo", [P, 2 * Q], F32)
        own_hi = tile("own_hi", [P, 2 * Q], F32)

        nc.sync.dma_start(key_pool[0][:], key_planes[0])
        nc.sync.dma_start(offsets[:], offs)
        nc.scalar.dma_start(size_cols[:], size[0].rearrange("(p c) -> p c", c=PACK))
        with nc.allow_non_contiguous_dma(reason="one gate value a partition"):
            nc.scalar.dma_start(gate_in[:], gb[0].rearrange("(m p) -> p m", p=P))
        for j in range(1, PACK):
            nc.sync.dma_start(key_pool[j][:], key_planes[j])
        nc.sync.dma_start(query_raw[:], query.rearrange("(p t) q -> p t q", t=PACK))
        nc.sync.dma_start(memq_raw[:], memq.rearrange("(p t) q -> p t q", t=PACK))
        nc.sync.dma_start(state_raw[0][:], state_pairs[0])
        nc.sync.dma_start(val_pool[0][:], val_planes[0])
        nc.sync.dma_start(state_raw[1][:], state_pairs[1])
        for j in range(1, PACK):
            nc.sync.dma_start(val_pool[j][:], val_planes[j])
        own_rows = own.rearrange("(p j) q -> p (j q)", j=PACK)
        nc.sync.dma_start(own_lo[:], own_rows[:, 0 : 2 * Q])
        nc.sync.dma_start(own_hi[:], own_rows[:, 2 * Q : 4 * Q])

        ident = tile("ident", [P, P], F32)
        make_identity(nc, ident[:])

        gate_clip = tile("gate_clip", [P, QT], F32)
        gate_exp = tile("gate_exp", [P, QT], F32)
        gate_den = tile("gate_den", [P, QT], F32)
        gate = tile("gate", [P, QT], F32)
        gate_rest = tile("gate_rest", [P, QT], F32)
        nc.vector.tensor_scalar(gate_clip[:], gate_in[:], GATE_FLOOR, None, ALU.max)
        nc.scalar.activation(gate_exp[:], gate_clip[:], ACT.Exp, scale=-1.0)
        nc.vector.tensor_scalar(gate_den[:], gate_exp[:], 1.0, None, ALU.add)
        nc.vector.reciprocal(gate[:], gate_den[:])
        nc.vector.tensor_tensor(gate_rest[:], gate_exp[:], gate[:], ALU.mult)

        size_rows = ps.tile([P, PACK, P], F32, name="size_rows", tag="bank_a")
        for c in range(PACK):
            nc.tensor.transpose(size_rows[:, c, :], size_cols[:, c : c + 1].to_broadcast([P, P]), ident[:])

        key_picked = tile("key_picked", [P, PACK, I], BF16)
        for j in range(PACK):
            nc.vector.tensor_copy(key_picked[:, j, :], key_pool[j][:].indirect(offsets[:]))
        key_woven = tile("key_woven", [P, I * PACK], BF16)
        key_slots = key_woven[:].rearrange("p (i t) -> p i t", t=PACK)
        for engine_copy, pair in ((nc.scalar.copy, slice(0, 2)), (nc.vector.tensor_copy, slice(2, 4))):
            engine_copy(out=key_slots[:, :, pair], in_=key_picked[:, pair, :].rearrange("p t i -> p i t"))
        query_mx = []
        for m, reuse in enumerate(("key_pool3", "key_picked")):
            query_woven = tile("query_woven%d" % m, [P, P * PACK], BF16)
            weave(nc.scalar.copy, query_woven[:], query_raw[:, :, m * P : (m + 1) * P])
            query_mx.append(mx_tiles("query%d" % m, P, reuse))
            quantize(query_mx[m], slice(0, P), query_woven[:])
            if m == 0:
                key_mx = mx_tiles("key", I)
                quantize(key_mx, slice(0, I), key_woven[:])

        memq_woven = tile("memq_woven", [P, Q * PACK], BF16)
        weave(nc.scalar.copy, memq_woven[:], memq_raw[:])
        state_woven = tile("state_woven", [P, E, PACK], BF16)

        def weave_pair(u):
            nc.scalar.copy(out=state_woven[:, :, 2 * u : 2 * u + 2], in_=state_raw[u][:].rearrange("p t e -> p e t"))

        weave_pair(0)
        row_sum = tile("row_sum", [P, QT], F32)
        probs_both = tile("probs", [P, QT, I], F32, "state_raw0")
        probs = [probs_both[:, m, :] for m in range(QT)]
        for m in range(QT):
            scores = ps.tile([P, I], F32, name="scores%d" % m, tag="bank_b%d" % m)
            matmul(scores[:], query_mx[m], slice(0, P), key_mx, slice(0, I))
            neg_max = tile("neg_max%d" % m, [P, 1], F32)
            nc.vector.tensor_reduce(neg_max[:], scores[:], AXIS.X, ALU.max, negate=True)
            nc.scalar.activation(probs[m][:], scores[:], ACT.Exp, bias=neg_max[:], accum_out=row_sum[:, m : m + 1])

        weave_pair(1)

        def pick(j, reuse=None):
            val_picked = tile("val_picked%d" % j, [P, I], BF16, reuse)
            nc.vector.tensor_copy(val_picked[:], val_pool[j][:].indirect(offsets[:]))
            return val_picked

        def turn_values(j, val_picked, woven):
            turned = ps.tile([P, 2, P], F32, name="turned_v%d" % j, tag=("bank_o", "bank_t1", "bank_t0", "bank_t1")[j])
            turn(turned, val_picked[:], woven)

        picked0 = pick(0)
        inv_sum = in_pool(0, 4096, "inv_sum", [P, QT], F32)
        nc.vector.reciprocal(inv_sum[:], row_sum[:])
        memq_mx = mx_tiles("memq", Q, pool=0)
        quantize(memq_mx, slice(0, Q), memq_woven[:])
        turned_woven = tile("turned_woven", [P, (Q + 2 * P) * PACK], BF16, "state_raw1")
        weight_woven = turned_woven[:, 0 : Q * PACK]
        for m in range(QT):
            weights = tile("weights%d" % m, [P, I], BF16)
            nc.vector.scalar_tensor_tensor(
                weights[:].rearrange("p (s c) -> p s c", c=PACK),
                probs[m][:].rearrange("p (s c) -> p s c", c=PACK),
                inv_sum[:, m : m + 1],
                size_rows[:].rearrange("p c s -> p s c"),
                ALU.mult,
                ALU.mult,
            )
            turned = ps.tile([P, 2, P], F32, name="turned_w%d" % m, tag="bank_t%d" % (m % 2))
            turn(turned, weights[:], weight_woven[:, m * P * PACK : (m + 1) * P * PACK])

        state_mx = mx_tiles("state", E)
        quantize(state_mx, slice(0, E), state_woven[:].rearrange("p e t -> p (e t)"))
        picked1 = pick(1)
        weight_mx = mx_tiles("weight", Q, pool=1)
        quantize(weight_mx, slice(0, Q), weight_woven[:])
        woven01 = turned_woven[:, Q * PACK : (Q + 2 * P) * PACK]
        turn_values(0, picked0, woven01[:, 0 : P * PACK])
        turn_values(1, picked1, woven01[:, P * PACK : 2 * P * PACK])

        result = tile("result", [P, PACK, X], F32)

        def attend(name, val_woven, width, val_mx, bank):
            quantize(val_mx, slice(0, width), val_woven[:])
            attn = ps.tile([P, QT, width], F32, name=name + "_attn", tag=bank)
            for m in range(QT):
                matmul(attn[:, m, :], weight_mx, slice(m * P, (m + 1) * P), val_mx, slice(0, width))
            return attn

        def gate_attn(attn, attn_gated):
            for m in range(QT):
                nc.scalar.activation(attn_gated[:, m, :], attn[:, m, :], ACT.Copy, scale=gate[:, m : m + 1])

        mem_reads = []
        for m in range(QT):
            mem_reads.append(ps.tile([P, E], F32, name="mem_read%d" % m, tag="bank_b%d" % m))
            matmul(mem_reads[m][:], memq_mx, slice(m * P, (m + 1) * P), state_mx, slice(0, E))

        def add_turned(mixed, block, start, stop):
            nc.tensor.matmul(mixed, block, ident[:], start=start, stop=stop, is_transpose=True)

        def mask(name, mixed, own_part, reuse):
            masked = tile(name, list(mixed.shape), F32, reuse)
            nc.vector.tensor_tensor(masked[:], mixed, own_part, ALU.mult)
            return masked

        def place_sums(masked, sums):
            nc.vector.tensor_reduce(sums, masked.rearrange("p (x k) -> p x k", k=Q // X), AXIS.X, ALU.add)

        picked2 = pick(2)
        woven2 = tile("val_woven2", [P, P * PACK], BF16)
        turn_values(2, picked2, woven2[:])
        attn01 = attend("val01", woven01, 2 * P, mx_tiles("val01", 2 * P, pool=2), "bank_o")
        mixed01 = ps.tile([P, 2, Q], F32, name="mixed01", tag="bank_a")
        mixed2 = ps.tile([P, Q], F32, name="mixed2", tag="bank_c2")
        mixed3 = ps.tile([P, Q], F32, name="mixed3", tag="bank_c3")
        mixed = [mixed01[:, 0, :], mixed01[:, 1, :], mixed2[:], mixed3[:]]
        for m in range(QT):
            mem_gated = tile("mem_gated0", [P, PACK, P], F32) if m == 0 else in_pool(2, 2048, "mem_gated1", [P, PACK, P], F32)
            nc.scalar.activation(
                mem_gated[:], mem_reads[m][:].rearrange("q (p j) -> q j p", j=PACK), ACT.Copy, scale=gate_rest[:, m : m + 1]
            )
            for j in range(PACK):
                add_turned(mixed[j][:, m * P : (m + 1) * P], mem_gated[:, j, :], m == 0 and j != 1, False)
        picked3 = pick(3)
        woven3 = tile("val_woven3", [P, P * PACK], BF16)
        turn_values(3, picked3, woven3[:])
        gated01 = in_pool(3, 4 * P, "gated01", [P, QT, 2 * P], F32)
        gate_attn(attn01, gated01)
        attn2 = attend("val2", woven2, P, mx_tiles("val2", P, pool=3), "bank_b0")
        val3_mx = mx_tiles("val3", P)
        quantize(val3_mx, slice(0, P), woven3[:])
        attn3 = [ps.tile([P, P], F32, name="attn3_%d" % m, tag=("bank_b1", "bank_t0")[m]) for m in range(QT)]
        for m in range(QT):
            matmul(attn3[m][:], weight_mx, slice(m * P, (m + 1) * P), val3_mx, slice(0, P))
        gated2 = tile("gated2", [P, QT, P], F32, "val_woven3")
        gate_attn(attn2, gated2)
        gated3 = tile("gated3", [P, QT, P], F32)
        for m in range(QT):
            nc.scalar.activation(gated3[:, m, :], attn3[m][:], ACT.Copy, scale=gate[:, m : m + 1])
        for m in range(QT):
            for j in range(2):
                add_turned(mixed[j][:, m * P : (m + 1) * P], gated01[:, m, j * P : (j + 1) * P], False, m == 1 and j == 1)
        masked01 = mask("masked01", mixed01[:].rearrange("p j q -> p (j q)"), own_lo[:], None)
        place_sums(masked01[:], result[:, 0:2, :].rearrange("p j x -> p (j x)"))
        out_rows = out.rearrange("(p j) x -> p j x", j=PACK)
        nc.sync.dma_start(out_rows[:, 0:2, :], result[:, 0:2, :])
        for j, gated in ((2, gated2), (3, gated3)):
            for m in range(QT):
                add_turned(mixed[j][:, m * P : (m + 1) * P], gated[:, m, :], False, m == 1)
            masked = mask("masked%d" % j, mixed[j], own_hi[:, (j - 2) * Q : (j - 1) * Q], None)
            place_sums(masked[:], result[:, j, :])
        nc.sync.dma_start(out_rows[:, 2:4, :], result[:, 2:4, :])
